import numpy as np
import ml_dtypes


def mxq(x, axis, fmt="e4m3"):
    dtype, down = {"e4m3": (ml_dtypes.float8_e4m3fn, 7), "e5m2": (ml_dtypes.float8_e5m2, 14)}[fmt]
    v = np.moveaxis(np.asarray(x, np.float32).astype(ml_dtypes.bfloat16).astype(np.float64), axis, -1)
    blocks = v.reshape(v.shape[:-1] + (-1, 32))
    amax = np.abs(blocks).max(-1, keepdims=True)
    byte = np.maximum(np.where(amax > 0, np.frexp(amax)[1] - 1 + 127, 0) - down, 1)
    scale = np.exp2(byte - 127.0)
    codes = (blocks / scale).astype(np.float32).astype(dtype).astype(np.float64)
    return np.moveaxis((codes * scale).reshape(v.shape), -1, axis)


WIDE = False


def mx_kscale(k):
    if not WIDE:
        return np.ones(k)
    levels = np.array([10, -10, 5, -5, 0])
    if k % 512:
        return np.exp2(np.random.permutation(np.resize(levels, k // 32))).repeat(32)
    a = np.empty((k // 512, 16))
    for p in range(k // 512):
        a[p, :8] = np.random.permutation(np.resize(levels, 8))
        for g in range(8):
            far = levels[np.abs(levels - a[p, g]) >= 10]
            a[p, g + 8] = far[np.random.randint(len(far))]
    return np.exp2(a.ravel()).repeat(32)


def f64(x):
    return np.asarray(x).astype(np.float64)


def striped(idx):
    return np.tile(idx.reshape(-1, 16).T, (8, 1)).astype(np.uint16)


def unstriped(offs):
    return offs[:16].T.reshape(-1).astype(np.int64)


E2M1 = np.array([0.0, 0.5, 1.0, 1.5, 2.0, 3.0, 4.0, 6.0, -0.0, -0.5, -1.0, -1.5, -2.0, -3.0, -4.0, -6.0])


def pack_weight(w, fmt):
    k, n = w.shape
    w = f64(np.asarray(w, np.float32).astype(ml_dtypes.bfloat16)).reshape(k // 32, 32, n)
    amax = np.abs(w).max(1)
    if fmt == "e4m3":
        byte = np.frexp(amax)[1] - 1 + 127 - 7
    else:
        mant, ex = np.frexp(amax / 6.0)
        byte = np.where(mant > 0.5, ex, ex - 1) + 127
    byte = np.clip(np.where(amax > 0, byte, 1), 1, 254)
    scaled = (w * np.exp2(127.0 - byte)[:, None, :]).reshape(k, n).astype(np.float32)
    by_word = np.ascontiguousarray(scaled.reshape(k // 512, 128, 4, n).transpose(0, 1, 3, 2))
    if fmt == "e4m3":
        words = by_word.astype(ml_dtypes.float8_e4m3fn).view(np.uint8)
    else:
        c = by_word.astype(ml_dtypes.float4_e2m1fn).view(np.uint8) & 0xF
        words = (c[..., 0::2] | (c[..., 1::2] << 4)).reshape(k // 512, 128, 2 * n)
    return np.ascontiguousarray(words), np.ascontiguousarray(byte.astype(np.uint8).reshape(k // 512, 16, n))


def unpack_weight(words, scales, fmt):
    g, _, n = scales.shape
    words = np.ascontiguousarray(words).reshape(g, 128, n, -1)
    if fmt == "e4m3":
        vals = words.view(ml_dtypes.float8_e4m3fn).astype(np.float64)
    else:
        nib = np.empty((g, 128, n, 4), np.uint8)
        nib[..., 0::2] = words & 0xF
        nib[..., 1::2] = words >> 4
        vals = E2M1[nib]
    vals = vals * np.repeat(np.exp2(scales.astype(np.float64) - 127.0), 8, axis=1)[..., None]
    return vals.transpose(0, 1, 3, 2).reshape(g * 512, n)


def pack_table(v):
    words, scales = pack_weight(v, "e4m3")
    return np.concatenate([words.reshape(words.shape[0], -1), scales.reshape(scales.shape[0], -1)], axis=1)


def unpack_table(tab):
    g, t = tab.shape[0], tab.shape[1] // 528
    return unpack_weight(tab[:, :512 * t].reshape(g, 128, t, 4), tab[:, 512 * t:].reshape(g, 16, t), "e4m3")


K, L, M, T, S = 1024, 1024, 256, 512, 256


def setup_inputs():
    n = np.random.standard_normal
    s1 = mx_kscale(K)[:, None]
    s2 = mx_kscale(L)[:, None]
    p_w4 = pack_weight(n((K, M)) / np.sqrt(K) / s1, "e2m1")
    return {
        "tab": pack_table(n((K, T)) * s1),
        "w4_words": p_w4[0],
        "w4_scales": p_w4[1],
        "tab2": pack_table(n((L, T)) * s2),
        "u": (n((L, M)) / np.sqrt(L) / s2).astype(np.float32),
        "offs": striped(np.random.permutation(T)[:S]),
        "offs2": striped(np.random.permutation(T)[:S]),
    }


def reference(tab, w4_words, w4_scales, tab2, u, offs, offs2):
    tab_ = unpack_table(tab)[:, unstriped(offs)]
    w4_ = unpack_weight(w4_words, w4_scales, "e2m1")
    tab2_ = unpack_table(tab2)[:, unstriped(offs2)]
    u_ = mxq(f64(u), 0, "e4m3")
    y = tab_.T @ w4_ + tab2_.T @ u_
    return y

@@ -1,0 +1,132 @@
+from contextlib import ExitStack
+
+import concourse.mybir as mybir
+
+K, M, T, S = 1024, 256, 512, 256
+P = 128
+PASSES = K // 512
+H = 128
+FLOPS = 2 * S * M * (K + K)
+
+F32 = mybir.dt.float32
+BF16 = mybir.dt.bfloat16
+I32 = mybir.dt.int32
+U32 = mybir.dt.uint32
+U16 = mybir.dt.uint16
+U8 = mybir.dt.uint8
+FP8X4 = mybir.dt.float8_e4m3fn_x4
+FP4X4 = mybir.dt.float4_e2m1fn_x4
+
+
+def tile_list_tab2_tm_none_kernel(tc, tab, w4_words, w4_scales, tab2, u, offs, offs2, out):
+    nc = tc.nc
+    with ExitStack() as ctx:
+        lists = ctx.enter_context(tc.tile_pool(name="lists", bufs=1))
+        held = ctx.enter_context(tc.tile_pool(name="held", bufs=1))
+        psum = ctx.enter_context(tc.psum_pool(name="psum", bufs=1))
+
+        idx = lists.tile([P, S // 16], U16, name="idx")
+        idx2 = lists.tile([P, S // 16], U16, name="idx2")
+
+        words = held.tile([P, PASSES * T], I32, name="words", align_bytes=64)
+        words2 = held.tile([P, PASSES * T], I32, name="words2", align_bytes=64)
+        rows = held.tile([P, PASSES * T // 4], I32, name="rows", align_bytes=64)
+        rows2 = held.tile([P, T // 4], I32, name="rows2", align_bytes=64)
+        w_words = held.tile([P, PASSES * M // 2], I32, name="w_words", align_bytes=64)
+        w_rows = held.tile([P, PASSES * M // 4], I32, name="w_rows", align_bytes=64)
+        raw = [held.tile([P, 4, M], F32, name=f"raw{a}", align_bytes=64) for a in range(PASSES)]
+        mixed = [held.tile([P, M, 4], BF16, name=f"mixed{a}", align_bytes=64) for a in range(PASSES)]
+        u_codes = [held.tile([P, M], U32, name=f"u_codes{a}", align_bytes=64) for a in range(PASSES)]
+        u_rows = [held.tile([P, M], U8, name=f"u_rows{a}", align_bytes=64) for a in range(PASSES)]
+        codes = [held.tile([P, S], U32, name=f"codes{a}", align_bytes=64) for a in range(PASSES)]
+        codes2 = [held.tile([P, S], U32, name=f"codes2_{a}", align_bytes=64) for a in range(PASSES)]
+        plane = [held.tile([P, S], U8, name=f"plane{a}", align_bytes=64) for a in range(PASSES)]
+        plane2 = held.tile([P, S], U8, name="plane2", align_bytes=64)
+
+        tab_words = tab[:, 0 : 512 * T].bitcast(I32).rearrange("a (p t) -> a p t", t=T)
+        tab_rows = tab[:, 512 * T : 528 * T].bitcast(I32).rearrange("a (q t) -> q a t", t=T // 4)
+        tab2_words = tab2[:, 0 : 512 * T].bitcast(I32).rearrange("a (p t) -> a p t", t=T)
+        tab2_rows = tab2[:, 512 * T : 528 * T].bitcast(I32).rearrange("a (q t) -> a q t", t=T // 4)
+        w4_rows = w4_scales.bitcast(I32).rearrange("a q n -> q a n")
+        nc.vector.memset(rows[:], 0)
+        nc.vector.memset(rows2[:], 0)
+        nc.gpsimd.memset(w_rows[:], 0)
+        nc.sync.dma_start(idx[:], offs)
+        nc.sync.dma_start(words[:, 0:T], tab_words[0])
+        for q in range(4):
+            nc.scalar.dma_start(
+                rows[32 * q : 32 * q + 4, :].rearrange("p (a t) -> p a t", a=PASSES), tab_rows[4 * q : 4 * q + 4]
+            )
+        nc.sync.dma_start(raw[0][:], u[0:512, :].rearrange("(p t) n -> p t n", t=4))
+        nc.sync.dma_start(words[:, T : 2 * T], tab_words[1])
+        nc.sync.dma_start(idx2[:], offs2)
+        nc.sync.dma_start(raw[1][:], u[512:1024, :].rearrange("(p t) n -> p t n", t=4))
+        for q in range(4):
+            nc.sync.dma_start(rows2[32 * q : 32 * q + 8, :], tab2_rows[:, 4 * q : 4 * q + 4, :])
+        for a in range(PASSES):
+            nc.sync.dma_start(words2[:, a * T : (a + 1) * T], tab2_words[a])
+        for q in range(4):
+            nc.gpsimd.dma_start(
+                w_rows[32 * q : 32 * q + 4, :].rearrange("p (a n) -> p a n", a=PASSES), w4_rows[4 * q : 4 * q + 4]
+            )
+        nc.gpsimd.dma_start(
+            w_words[:].rearrange("p (a b) -> p a b", a=PASSES), w4_words.bitcast(I32).rearrange("a p b -> p a b")
+        )
+
+        nc.vector.tensor_copy(codes[0][:], words[:, 0:T].bitcast(U32).indirect(idx[:]))
+        for a in range(PASSES):
+            nc.vector.tensor_copy(plane[a][:], rows[:].bitcast(U8)[:, a * T : (a + 1) * T].indirect(idx[:]))
+        nc.vector.tensor_copy(codes[1][:], words[:, T : 2 * T].bitcast(U32).indirect(idx[:]))
+
+        for a in range(PASSES):
+            nc.scalar.copy(
+                out=mixed[a][:].rearrange("p (c i) t -> p c t i", i=4),
+                in_=raw[a][:].rearrange("p t (c i) -> p c t i", i=4),
+            )
+        nc.vector.tensor_copy(plane2[:], rows2[:].bitcast(U8).indirect(idx2[:]))
+        nc.vector.quantize_mx(
+            out=u_codes[0][:].bitcast(FP8X4), scales=u_rows[0][:], in_=mixed[0][:].rearrange("p n t -> p (n t)")
+        )
+        nc.vector.tensor_copy(codes2[0][:], words2[:, 0:T].bitcast(U32).indirect(idx2[:]))
+        nc.vector.quantize_mx(
+            out=u_codes[1][:].bitcast(FP8X4), scales=u_rows[1][:], in_=mixed[1][:].rearrange("p n t -> p (n t)")
+        )
+        for j in range(2):
+            nc.vector.tensor_copy(
+                codes2[1][:, j * H : (j + 1) * H], words2[:, T : 2 * T].bitcast(U32).indirect(idx2[:, 8 * j : 8 * j + 8])
+            )
+
+        sums = [psum.tile([P, H], F32, name=f"sums{g}") for g in range(4)]
+        w_bytes = w_words[:].bitcast(U8)
+        w_planes = w_rows[:].bitcast(U8)
+        for a in range(PASSES):
+            for g in range(4):
+                j, n = (g // 2) * H, (g % 2) * H
+                nc.tensor.matmul_mx(
+                    out=sums[g][:],
+                    lhsT=codes[a][:, j : j + H].bitcast(FP8X4),
+                    lhsT_scale=plane[a][:, j : j + H],
+                    rhs=w_bytes[:, 2 * (a * M + n) : 2 * (a * M + n + H)].bitcast(FP4X4),
+                    rhs_scale=w_planes[:, a * M + n : a * M + n + H],
+                    start=(a == 0),
+                    stop=False,
+                )
+        for a in range(PASSES):
+            for g in range(4):
+                j, n = (g // 2) * H, (g % 2) * H
+                nc.tensor.matmul_mx(
+                    out=sums[g][:],
+                    lhsT=codes2[a][:, j : j + H].bitcast(FP8X4),
+                    lhsT_scale=plane2[4 * a : P, j : j + H],
+                    rhs=u_codes[a][:, n : n + H].bitcast(FP8X4),
+                    rhs_scale=u_rows[a][:, n : n + H],
+                    start=False,
+                    stop=(a == PASSES - 1),
+                )
+        result = [held.tile([P, M], F32, name=f"result{j}", align_bytes=64) for j in range(2)]
+        nc.scalar.copy(out=result[0][:, 0:H], in_=sums[0][:])
+        nc.scalar.copy(out=result[0][:, H : 2 * H], in_=sums[1][:])
+        nc.sync.dma_start(out[0:H, :], result[0][:])
+        nc.scalar.copy(out=result[1][:, 0:H], in_=sums[2][:])
+        nc.vector.tensor_copy(out=result[1][:, H : 2 * H], in_=sums[3][:])
+        nc.sync.dma_start(out[H : 2 * H, :], result[1][:])

@@ -52,56 +52,60 @@ def tile_list_tab2_tm_none_kernel(tc, tab, w4_words, w4_scales, tab2, u, offs, o
         nc.vector.memset(rows2[:], 0)
         nc.gpsimd.memset(w_rows[:], 0)
         nc.sync.dma_start(idx[:], offs)
-        nc.sync.dma_start(words[:, 0:T], tab_words[0])
+        nc.sync.dma_start(idx2[:], offs2)
         for q in range(4):
             nc.scalar.dma_start(
                 rows[32 * q : 32 * q + 4, :].rearrange("p (a t) -> p a t", a=PASSES), tab_rows[4 * q : 4 * q + 4]
             )
+        nc.sync.dma_start(words[:].rearrange("p (a t) -> p a t", a=PASSES), tab_words.rearrange("a p t -> p a t"))
         nc.sync.dma_start(raw[0][:], u[0:512, :].rearrange("(p t) n -> p t n", t=4))
-        nc.sync.dma_start(words[:, T : 2 * T], tab_words[1])
-        nc.sync.dma_start(idx2[:], offs2)
+        nc.sync.dma_start(words2[:, 0:T], tab2_words[0])
+        nc.sync.dma_start(
+            w_words[:].rearrange("p (a b) -> p a b", a=PASSES), w4_words.bitcast(I32).rearrange("a p b -> p a b")
+        )
         nc.sync.dma_start(raw[1][:], u[512:1024, :].rearrange("(p t) n -> p t n", t=4))
         for q in range(4):
             nc.sync.dma_start(rows2[32 * q : 32 * q + 8, :], tab2_rows[:, 4 * q : 4 * q + 4, :])
-        for a in range(PASSES):
-            nc.sync.dma_start(words2[:, a * T : (a + 1) * T], tab2_words[a])
         for q in range(4):
             nc.gpsimd.dma_start(
                 w_rows[32 * q : 32 * q + 4, :].rearrange("p (a n) -> p a n", a=PASSES), w4_rows[4 * q : 4 * q + 4]
             )
-        nc.gpsimd.dma_start(
-            w_words[:].rearrange("p (a b) -> p a b", a=PASSES), w4_words.bitcast(I32).rearrange("a p b -> p a b")
-        )
+        nc.sync.dma_start(words2[:, T : 2 * T], tab2_words[1])
 
-        nc.vector.tensor_copy(codes[0][:], words[:, 0:T].bitcast(U32).indirect(idx[:]))
         for a in range(PASSES):
             nc.vector.tensor_copy(plane[a][:], rows[:].bitcast(U8)[:, a * T : (a + 1) * T].indirect(idx[:]))
-        nc.vector.tensor_copy(codes[1][:], words[:, T : 2 * T].bitcast(U32).indirect(idx[:]))
-
         for a in range(PASSES):
+            nc.vector.tensor_copy(codes[a][:], words[:, a * T : (a + 1) * T].bitcast(U32).indirect(idx[:]))
+
+        def interleave(a, n0, n1):
             nc.scalar.copy(
-                out=mixed[a][:].rearrange("p (c i) t -> p c t i", i=4),
-                in_=raw[a][:].rearrange("p t (c i) -> p c t i", i=4),
+                out=mixed[a][:, n0:n1, :].rearrange("p (c i) t -> p c t i", i=4),
+                in_=raw[a][:, :, n0:n1].rearrange("p t (c i) -> p c t i", i=4),
             )
-        nc.vector.tensor_copy(plane2[:], rows2[:].bitcast(U8).indirect(idx2[:]))
-        nc.vector.quantize_mx(
-            out=u_codes[0][:].bitcast(FP8X4), scales=u_rows[0][:], in_=mixed[0][:].rearrange("p n t -> p (n t)")
-        )
+
+        def quantize(a, n0, n1):
+            nc.vector.quantize_mx(
+                out=u_codes[a][:, n0:n1].bitcast(FP8X4),
+                scales=u_rows[a][:, n0:n1],
+                in_=mixed[a][:, n0:n1, :].rearrange("p n t -> p (n t)"),
+            )
+
+        interleave(0, 0, M)
+        quantize(0, 0, M)
         nc.vector.tensor_copy(codes2[0][:], words2[:, 0:T].bitcast(U32).indirect(idx2[:]))
-        nc.vector.quantize_mx(
-            out=u_codes[1][:].bitcast(FP8X4), scales=u_rows[1][:], in_=mixed[1][:].rearrange("p n t -> p (n t)")
-        )
-        for j in range(2):
-            nc.vector.tensor_copy(
-                codes2[1][:, j * H : (j + 1) * H], words2[:, T : 2 * T].bitcast(U32).indirect(idx2[:, 8 * j : 8 * j + 8])
-            )
+        interleave(1, 0, H)
+        interleave(1, H, M)
+        nc.vector.tensor_copy(plane2[:], rows2[:].bitcast(U8).indirect(idx2[:]))
+        nc.vector.tensor_copy(codes2[1][:], words2[:, T : 2 * T].bitcast(U32).indirect(idx2[:]))
+        quantize(1, 0, H)
+        quantize(1, H, M)
 
         sums = [psum.tile([P, H], F32, name=f"sums{g}") for g in range(4)]
         w_bytes = w_words[:].bitcast(U8)
         w_planes = w_rows[:].bitcast(U8)
         for a in range(PASSES):
             for g in range(4):
-                j, n = (g // 2) * H, (g % 2) * H
+                j, n = (g % 2) * H, (g // 2) * H
                 nc.tensor.matmul_mx(
                     out=sums[g][:],
                     lhsT=codes[a][:, j : j + H].bitcast(FP8X4),
@@ -113,7 +117,7 @@ def tile_list_tab2_tm_none_kernel(tc, tab, w4_words, w4_scales, tab2, u, offs, o
                 )
         for a in range(PASSES):
             for g in range(4):
-                j, n = (g // 2) * H, (g % 2) * H
+                j, n = (g % 2) * H, (g // 2) * H
                 nc.tensor.matmul_mx(
                     out=sums[g][:],
                     lhsT=codes2[a][:, j : j + H].bitcast(FP8X4),
@@ -124,9 +128,9 @@ def tile_list_tab2_tm_none_kernel(tc, tab, w4_words, w4_scales, tab2, u, offs, o
                     stop=(a == PASSES - 1),
                 )
         result = [held.tile([P, M], F32, name=f"result{j}", align_bytes=64) for j in range(2)]
-        nc.scalar.copy(out=result[0][:, 0:H], in_=sums[0][:])
-        nc.scalar.copy(out=result[0][:, H : 2 * H], in_=sums[1][:])
+        for h in range(2):
+            cols = slice(h * H, (h + 1) * H)
+            nc.scalar.copy(out=result[0][:, cols], in_=sums[2 * h][:])
+            nc.vector.tensor_copy(out=result[1][:, cols], in_=sums[2 * h + 1][:])
         nc.sync.dma_start(out[0:H, :], result[0][:])
-        nc.scalar.copy(out=result[1][:, 0:H], in_=sums[2][:])
-        nc.vector.tensor_copy(out=result[1][:, H : 2 * H], in_=sums[3][:])
         nc.sync.dma_start(out[H : 2 * H, :], result[1][:])

@@ -52,30 +52,29 @@ def tile_list_tab2_tm_none_kernel(tc, tab, w4_words, w4_scales, tab2, u, offs, o
         nc.vector.memset(rows2[:], 0)
         nc.gpsimd.memset(w_rows[:], 0)
         nc.sync.dma_start(idx[:], offs)
-        nc.sync.dma_start(idx2[:], offs2)
+        nc.sync.dma_start(words[:].rearrange("p (a t) -> p a t", a=PASSES), tab_words.rearrange("a p t -> p a t"))
         for q in range(4):
-            nc.scalar.dma_start(
+            nc.sync.dma_start(
                 rows[32 * q : 32 * q + 4, :].rearrange("p (a t) -> p a t", a=PASSES), tab_rows[4 * q : 4 * q + 4]
             )
-        nc.sync.dma_start(words[:].rearrange("p (a t) -> p a t", a=PASSES), tab_words.rearrange("a p t -> p a t"))
-        nc.sync.dma_start(raw[0][:], u[0:512, :].rearrange("(p t) n -> p t n", t=4))
-        nc.sync.dma_start(words2[:, 0:T], tab2_words[0])
-        nc.sync.dma_start(
-            w_words[:].rearrange("p (a b) -> p a b", a=PASSES), w4_words.bitcast(I32).rearrange("a p b -> p a b")
-        )
-        nc.sync.dma_start(raw[1][:], u[512:1024, :].rearrange("(p t) n -> p t n", t=4))
-        for q in range(4):
-            nc.sync.dma_start(rows2[32 * q : 32 * q + 8, :], tab2_rows[:, 4 * q : 4 * q + 4, :])
         for q in range(4):
             nc.gpsimd.dma_start(
                 w_rows[32 * q : 32 * q + 4, :].rearrange("p (a n) -> p a n", a=PASSES), w4_rows[4 * q : 4 * q + 4]
             )
-        nc.sync.dma_start(words2[:, T : 2 * T], tab2_words[1])
+        for a in range(PASSES):
+            nc.sync.dma_start(raw[a][:], u[512 * a : 512 * a + 512, :].rearrange("(p t) n -> p t n", t=4))
+        nc.sync.dma_start(idx2[:], offs2)
+        nc.sync.dma_start(words2[:].rearrange("p (a t) -> p a t", a=PASSES), tab2_words.rearrange("a p t -> p a t"))
+        nc.sync.dma_start(
+            w_words[:].rearrange("p (a b) -> p a b", a=PASSES), w4_words.bitcast(I32).rearrange("a p b -> p a b")
+        )
+        for q in range(4):
+            nc.sync.dma_start(rows2[32 * q : 32 * q + 8, :], tab2_rows[:, 4 * q : 4 * q + 4, :])
 
         for a in range(PASSES):
-            nc.vector.tensor_copy(plane[a][:], rows[:].bitcast(U8)[:, a * T : (a + 1) * T].indirect(idx[:]))
-        for a in range(PASSES):
             nc.vector.tensor_copy(codes[a][:], words[:, a * T : (a + 1) * T].bitcast(U32).indirect(idx[:]))
+        for a in range(PASSES):
+            nc.vector.tensor_copy(plane[a][:], rows[:].bitcast(U8)[:, a * T : (a + 1) * T].indirect(idx[:]))
 
         def interleave(a, n0, n1):
             nc.scalar.copy(
@@ -91,21 +90,22 @@ def tile_list_tab2_tm_none_kernel(tc, tab, w4_words, w4_scales, tab2, u, offs, o
             )
 
         interleave(0, 0, M)
+        interleave(1, 0, M)
         quantize(0, 0, M)
         nc.vector.tensor_copy(codes2[0][:], words2[:, 0:T].bitcast(U32).indirect(idx2[:]))
-        interleave(1, 0, H)
-        interleave(1, H, M)
         nc.vector.tensor_copy(plane2[:], rows2[:].bitcast(U8).indirect(idx2[:]))
-        nc.vector.tensor_copy(codes2[1][:], words2[:, T : 2 * T].bitcast(U32).indirect(idx2[:]))
-        quantize(1, 0, H)
-        quantize(1, H, M)
+        quantize(1, 0, M)
+        for j in range(2):
+            nc.vector.tensor_copy(
+                codes2[1][:, j * H : (j + 1) * H], words2[:, T : 2 * T].bitcast(U32).indirect(idx2[:, 8 * j : 8 * j + 8])
+            )
 
         sums = [psum.tile([P, H], F32, name=f"sums{g}") for g in range(4)]
         w_bytes = w_words[:].bitcast(U8)
         w_planes = w_rows[:].bitcast(U8)
         for a in range(PASSES):
             for g in range(4):
-                j, n = (g % 2) * H, (g // 2) * H
+                j, n = (g // 2) * H, (g % 2) * H
                 nc.tensor.matmul_mx(
                     out=sums[g][:],
                     lhsT=codes[a][:, j : j + H].bitcast(FP8X4),
@@ -117,7 +117,7 @@ def tile_list_tab2_tm_none_kernel(tc, tab, w4_words, w4_scales, tab2, u, offs, o
                 )
         for a in range(PASSES):
             for g in range(4):
-                j, n = (g % 2) * H, (g // 2) * H
+                j, n = (g // 2) * H, (g % 2) * H
                 nc.tensor.matmul_mx(
                     out=sums[g][:],
                     lhsT=codes2[a][:, j : j + H].bitcast(FP8X4),
@@ -128,9 +128,9 @@ def tile_list_tab2_tm_none_kernel(tc, tab, w4_words, w4_scales, tab2, u, offs, o
                     stop=(a == PASSES - 1),
                 )
         result = [held.tile([P, M], F32, name=f"result{j}", align_bytes=64) for j in range(2)]
-        for h in range(2):
-            cols = slice(h * H, (h + 1) * H)
-            nc.scalar.copy(out=result[0][:, cols], in_=sums[2 * h][:])
-            nc.vector.tensor_copy(out=result[1][:, cols], in_=sums[2 * h + 1][:])
+        nc.scalar.copy(out=result[0][:, 0:H], in_=sums[0][:])
+        nc.scalar.copy(out=result[0][:, H:M], in_=sums[1][:])
         nc.sync.dma_start(out[0:H, :], result[0][:])
+        nc.scalar.copy(out=result[1][:, 0:H], in_=sums[2][:])
+        nc.vector.tensor_copy(out=result[1][:, H:M], in_=sums[3][:])
         nc.sync.dma_start(out[H : 2 * H, :], result[1][:])

@@ -52,28 +52,33 @@ def tile_list_tab2_tm_none_kernel(tc, tab, w4_words, w4_scales, tab2, u, offs, o
         nc.vector.memset(rows2[:], 0)
         nc.gpsimd.memset(w_rows[:], 0)
         nc.sync.dma_start(idx[:], offs)
-        nc.sync.dma_start(words[:].rearrange("p (a t) -> p a t", a=PASSES), tab_words.rearrange("a p t -> p a t"))
+        def load_w_rows(engine, q):
+            engine.dma_start(
+                w_rows[32 * q : 32 * q + 4, :].rearrange("p (a n) -> p a n", a=PASSES), w4_rows[4 * q : 4 * q + 4]
+            )
+
+        for q in range(3):
+            load_w_rows(nc.gpsimd, q)
+        nc.sync.dma_start(words[:, 0:T], tab_words[0])
         for q in range(4):
             nc.sync.dma_start(
                 rows[32 * q : 32 * q + 4, :].rearrange("p (a t) -> p a t", a=PASSES), tab_rows[4 * q : 4 * q + 4]
             )
-        for q in range(4):
-            nc.gpsimd.dma_start(
-                w_rows[32 * q : 32 * q + 4, :].rearrange("p (a n) -> p a n", a=PASSES), w4_rows[4 * q : 4 * q + 4]
-            )
-        for a in range(PASSES):
-            nc.sync.dma_start(raw[a][:], u[512 * a : 512 * a + 512, :].rearrange("(p t) n -> p t n", t=4))
+        nc.sync.dma_start(words[:, T : 2 * T], tab_words[1])
+        nc.sync.dma_start(raw[0][:], u[0:512, :].rearrange("(p t) n -> p t n", t=4))
         nc.sync.dma_start(idx2[:], offs2)
-        nc.sync.dma_start(words2[:].rearrange("p (a t) -> p a t", a=PASSES), tab2_words.rearrange("a p t -> p a t"))
+        nc.sync.dma_start(words2[:, 0:T], tab2_words[0])
+        load_w_rows(nc.sync, 3)
+        nc.sync.dma_start(raw[1][:], u[512:1024, :].rearrange("(p t) n -> p t n", t=4))
         nc.sync.dma_start(
             w_words[:].rearrange("p (a b) -> p a b", a=PASSES), w4_words.bitcast(I32).rearrange("a p b -> p a b")
         )
         for q in range(4):
             nc.sync.dma_start(rows2[32 * q : 32 * q + 8, :], tab2_rows[:, 4 * q : 4 * q + 4, :])
+        nc.sync.dma_start(words2[:, T : 2 * T], tab2_words[1])
 
         for a in range(PASSES):
             nc.vector.tensor_copy(codes[a][:], words[:, a * T : (a + 1) * T].bitcast(U32).indirect(idx[:]))
-        for a in range(PASSES):
             nc.vector.tensor_copy(plane[a][:], rows[:].bitcast(U8)[:, a * T : (a + 1) * T].indirect(idx[:]))
 
         def interleave(a, n0, n1):
@@ -90,15 +95,26 @@ def tile_list_tab2_tm_none_kernel(tc, tab, w4_words, w4_scales, tab2, u, offs, o
             )
 
         interleave(0, 0, M)
-        interleave(1, 0, M)
-        quantize(0, 0, M)
-        nc.vector.tensor_copy(codes2[0][:], words2[:, 0:T].bitcast(U32).indirect(idx2[:]))
-        nc.vector.tensor_copy(plane2[:], rows2[:].bitcast(U8).indirect(idx2[:]))
-        quantize(1, 0, M)
-        for j in range(2):
+        interleave(1, 0, H)
+        nc.gpsimd.tensor_scalar(
+            out=mixed[1][:, H:M, :].rearrange("p (c i) t -> p c t i", i=4),
+            in0=raw[1][:, :, H:M].rearrange("p t (c i) -> p c t i", i=4),
+            scalar1=1.0,
+            scalar2=0.0,
+            op0=mybir.AluOpType.mult,
+            op1=mybir.AluOpType.add,
+        )
+        def gather2(j):
             nc.vector.tensor_copy(
                 codes2[1][:, j * H : (j + 1) * H], words2[:, T : 2 * T].bitcast(U32).indirect(idx2[:, 8 * j : 8 * j + 8])
             )
+
+        nc.vector.tensor_copy(codes2[0][:], words2[:, 0:T].bitcast(U32).indirect(idx2[:]))
+        quantize(0, 0, M)
+        nc.vector.tensor_copy(plane2[:], rows2[:].bitcast(U8).indirect(idx2[:]))
+        quantize(1, 0, M)
+        gather2(0)
+        gather2(1)
 
         sums = [psum.tile([P, H], F32, name=f"sums{g}") for g in range(4)]
         w_bytes = w_words[:].bitcast(U8)

from contextlib import ExitStack

import concourse.mybir as mybir

K, M, T, S = 1024, 256, 512, 256
P = 128
PASSES = K // 512
H = 128
FLOPS = 2 * S * M * (K + K)

F32 = mybir.dt.float32
BF16 = mybir.dt.bfloat16
I32 = mybir.dt.int32
U32 = mybir.dt.uint32
U16 = mybir.dt.uint16
U8 = mybir.dt.uint8
FP8X4 = mybir.dt.float8_e4m3fn_x4
FP4X4 = mybir.dt.float4_e2m1fn_x4


def tile_list_tab2_tm_none_kernel(tc, tab, w4_words, w4_scales, tab2, u, offs, offs2, out):
    nc = tc.nc
    with ExitStack() as ctx:
        lists = ctx.enter_context(tc.tile_pool(name="lists", bufs=1))
        held = ctx.enter_context(tc.tile_pool(name="held", bufs=1))
        psum = ctx.enter_context(tc.psum_pool(name="psum", bufs=1))

        idx = lists.tile([P, S // 16], U16, name="idx")
        idx2 = lists.tile([P, S // 16], U16, name="idx2")

        words = held.tile([P, PASSES * T], I32, name="words", align_bytes=64)
        words2 = held.tile([P, PASSES * T], I32, name="words2", align_bytes=64)
        rows = held.tile([P, PASSES * T // 4], I32, name="rows", align_bytes=64)
        rows2 = held.tile([P, T // 4], I32, name="rows2", align_bytes=64)
        w_words = held.tile([P, PASSES * M // 2], I32, name="w_words", align_bytes=64)
        w_rows = held.tile([P, PASSES * M // 4], I32, name="w_rows", align_bytes=64)
        raw = [held.tile([P, 4, M], F32, name=f"raw{a}", align_bytes=64) for a in range(PASSES)]
        mixed = [held.tile([P, M, 4], BF16, name=f"mixed{a}", align_bytes=64) for a in range(PASSES)]
        u_codes = [held.tile([P, M], U32, name=f"u_codes{a}", align_bytes=64) for a in range(PASSES)]
        u_rows = [held.tile([P, M], U8, name=f"u_rows{a}", align_bytes=64) for a in range(PASSES)]
        codes = [held.tile([P, S], U32, name=f"codes{a}", align_bytes=64) for a in range(PASSES)]
        codes2 = [held.tile([P, S], U32, name=f"codes2_{a}", align_bytes=64) for a in range(PASSES)]
        plane = [held.tile([P, S], U8, name=f"plane{a}", align_bytes=64) for a in range(PASSES)]
        plane2 = held.tile([P, S], U8, name="plane2", align_bytes=64)

        tab_words = tab[:, 0 : 512 * T].bitcast(I32).rearrange("a (p t) -> a p t", t=T)
        tab_rows = tab[:, 512 * T : 528 * T].bitcast(I32).rearrange("a (q t) -> q a t", t=T // 4)
        tab2_words = tab2[:, 0 : 512 * T].bitcast(I32).rearrange("a (p t) -> a p t", t=T)
        tab2_rows = tab2[:, 512 * T : 528 * T].bitcast(I32).rearrange("a (q t) -> a q t", t=T // 4)
        w4_rows = w4_scales.bitcast(I32).rearrange("a q n -> q a n")
        nc.vector.memset(rows[:], 0)
        nc.vector.memset(rows2[:], 0)
        nc.gpsimd.memset(w_rows[:], 0)
        nc.sync.dma_start(idx[:], offs)
        def load_w_rows(engine, q):
            engine.dma_start(
                w_rows[32 * q : 32 * q + 4, :].rearrange("p (a n) -> p a n", a=PASSES), w4_rows[4 * q : 4 * q + 4]
            )

        for q in range(3):
            load_w_rows(nc.gpsimd, q)
        nc.sync.dma_start(words[:, 0:T], tab_words[0])
        for q in range(4):
            nc.sync.dma_start(
                rows[32 * q : 32 * q + 4, :].rearrange("p (a t) -> p a t", a=PASSES), tab_rows[4 * q : 4 * q + 4]
            )
        nc.sync.dma_start(words[:, T : 2 * T], tab_words[1])
        nc.sync.dma_start(raw[0][:], u[0:512, :].rearrange("(p t) n -> p t n", t=4))
        nc.sync.dma_start(idx2[:], offs2)
        nc.sync.dma_start(words2[:, 0:T], tab2_words[0])
        load_w_rows(nc.sync, 3)
        nc.sync.dma_start(raw[1][:], u[512:1024, :].rearrange("(p t) n -> p t n", t=4))
        nc.sync.dma_start(
            w_words[:].rearrange("p (a b) -> p a b", a=PASSES), w4_words.bitcast(I32).rearrange("a p b -> p a b")
        )
        for q in range(4):
            nc.sync.dma_start(rows2[32 * q : 32 * q + 8, :], tab2_rows[:, 4 * q : 4 * q + 4, :])
        nc.sync.dma_start(words2[:, T : 2 * T], tab2_words[1])

        for a in range(PASSES):
            nc.vector.tensor_copy(codes[a][:], words[:, a * T : (a + 1) * T].bitcast(U32).indirect(idx[:]))
            nc.vector.tensor_copy(plane[a][:], rows[:].bitcast(U8)[:, a * T : (a + 1) * T].indirect(idx[:]))

        def interleave(a, n0, n1):
            nc.scalar.copy(
                out=mixed[a][:, n0:n1, :].rearrange("p (c i) t -> p c t i", i=4),
                in_=raw[a][:, :, n0:n1].rearrange("p t (c i) -> p c t i", i=4),
            )

        def quantize(a, n0, n1):
            nc.vector.quantize_mx(
                out=u_codes[a][:, n0:n1].bitcast(FP8X4),
                scales=u_rows[a][:, n0:n1],
                in_=mixed[a][:, n0:n1, :].rearrange("p n t -> p (n t)"),
            )

        interleave(0, 0, M)
        interleave(1, 0, H)
        nc.gpsimd.tensor_scalar(
            out=mixed[1][:, H:M, :].rearrange("p (c i) t -> p c t i", i=4),
            in0=raw[1][:, :, H:M].rearrange("p t (c i) -> p c t i", i=4),
            scalar1=1.0,
            scalar2=0.0,
            op0=mybir.AluOpType.mult,
            op1=mybir.AluOpType.add,
        )
        def gather2(j):
            nc.vector.tensor_copy(
                codes2[1][:, j * H : (j + 1) * H], words2[:, T : 2 * T].bitcast(U32).indirect(idx2[:, 8 * j : 8 * j + 8])
            )

        nc.vector.tensor_copy(codes2[0][:], words2[:, 0:T].bitcast(U32).indirect(idx2[:]))
        quantize(0, 0, M)
        nc.vector.tensor_copy(plane2[:], rows2[:].bitcast(U8).indirect(idx2[:]))
        quantize(1, 0, M)
        gather2(0)
        gather2(1)

        sums = [psum.tile([P, H], F32, name=f"sums{g}") for g in range(4)]
        w_bytes = w_words[:].bitcast(U8)
        w_planes = w_rows[:].bitcast(U8)
        for a in range(PASSES):
            for g in range(4):
                j, n = (g // 2) * H, (g % 2) * H
                nc.tensor.matmul_mx(
                    out=sums[g][:],
                    lhsT=codes[a][:, j : j + H].bitcast(FP8X4),
                    lhsT_scale=plane[a][:, j : j + H],
                    rhs=w_bytes[:, 2 * (a * M + n) : 2 * (a * M + n + H)].bitcast(FP4X4),
                    rhs_scale=w_planes[:, a * M + n : a * M + n + H],
                    start=(a == 0),
                    stop=False,
                )
        for a in range(PASSES):
            for g in range(4):
                j, n = (g // 2) * H, (g % 2) * H
                nc.tensor.matmul_mx(
                    out=sums[g][:],
                    lhsT=codes2[a][:, j : j + H].bitcast(FP8X4),
                    lhsT_scale=plane2[4 * a : P, j : j + H],
                    rhs=u_codes[a][:, n : n + H].bitcast(FP8X4),
                    rhs_scale=u_rows[a][:, n : n + H],
                    start=False,
                    stop=(a == PASSES - 1),
                )
        result = [held.tile([P, M], F32, name=f"result{j}", align_bytes=64) for j in range(2)]
        nc.scalar.copy(out=result[0][:, 0:H], in_=sums[0][:])
        nc.scalar.copy(out=result[0][:, H:M], in_=sums[1][:])
        nc.sync.dma_start(out[0:H, :], result[0][:])
        nc.scalar.copy(out=result[1][:, 0:H], in_=sums[2][:])
        nc.vector.tensor_copy(out=result[1][:, H:M], in_=sums[3][:])
        nc.sync.dma_start(out[H : 2 * H, :], result[1][:])
